import numpy as np
import ml_dtypes


def mxq(x, axis, fmt="e4m3"):
    dtype, down = {"e4m3": (ml_dtypes.float8_e4m3fn, 7), "e5m2": (ml_dtypes.float8_e5m2, 14)}[fmt]
    v = np.moveaxis(np.asarray(x, np.float32).astype(ml_dtypes.bfloat16).astype(np.float64), axis, -1)
    blocks = v.reshape(v.shape[:-1] + (-1, 32))
    amax = np.abs(blocks).max(-1, keepdims=True)
    byte = np.maximum(np.where(amax > 0, np.frexp(amax)[1] - 1 + 127, 0) - down, 1)
    scale = np.exp2(byte - 127.0)
    codes = (blocks / scale).astype(np.float32).astype(dtype).astype(np.float64)
    return np.moveaxis((codes * scale).reshape(v.shape), -1, axis)


WIDE = False


def mx_kscale(k):
    if not WIDE:
        return np.ones(k)
    levels = np.array([10, -10, 5, -5, 0])
    if k % 512:
        return np.exp2(np.random.permutation(np.resize(levels, k // 32))).repeat(32)
    a = np.empty((k // 512, 16))
    for p in range(k // 512):
        a[p, :8] = np.random.permutation(np.resize(levels, 8))
        for g in range(8):
            far = levels[np.abs(levels - a[p, g]) >= 10]
            a[p, g + 8] = far[np.random.randint(len(far))]
    return np.exp2(a.ravel()).repeat(32)


def f64(x):
    return np.asarray(x).astype(np.float64)


def striped(idx):
    return np.tile(idx.reshape(-1, 16).T, (8, 1)).astype(np.uint16)


def unstriped(offs):
    return offs[:16].T.reshape(-1).astype(np.int64)


def pack_weight(w):
    k, n = w.shape
    w = f64(np.asarray(w, np.float32).astype(ml_dtypes.bfloat16)).reshape(k // 32, 32, n)
    amax = np.abs(w).max(1)
    byte = np.clip(np.where(amax > 0, np.frexp(amax)[1] - 1 + 127 - 7, 1), 1, 254)
    scaled = (w * np.exp2(127.0 - byte)[:, None, :]).reshape(k, n).astype(np.float32)
    words = np.ascontiguousarray(scaled.reshape(k // 512, 128, 4, n).transpose(0, 1, 3, 2)).astype(ml_dtypes.float8_e4m3fn).view(np.uint8)
    return words, np.ascontiguousarray(byte.astype(np.uint8).reshape(k // 512, 16, n))


def unpack_weight(words, scales):
    g, p, n, _ = words.shape
    vals = np.ascontiguousarray(words).view(ml_dtypes.float8_e4m3fn).astype(np.float64) * np.repeat(np.exp2(scales.astype(np.float64) - 127.0), 8, axis=1)[..., None]
    return vals.transpose(0, 1, 3, 2).reshape(g * 512, n)


def sigmoid(v):
    return 1.0 / (1.0 + np.exp(-np.maximum(v, -700.0)))


K, T, S, N = 1024, 1024, 512, 128


def setup_inputs():
    n = np.random.standard_normal
    s = mx_kscale(K)[:, None]
    packed_xT = pack_weight(n((K, T)) * s)
    return {
        "x_words": packed_xT[0],
        "x_scales": packed_xT[1],
        "w1": (n((K, N)) / np.sqrt(K) / s).astype(np.float32),
        "w2": (n((K, N)) / np.sqrt(K) / s).astype(np.float32),
        "w3": (n((K, N)) / np.sqrt(K) / s).astype(np.float32),
        "wc2": (n((N, 1))).astype(np.float32),
        "bg2": (0.5 * n((N, 1))).astype(np.float32),
        "offs": striped(np.random.permutation(T)[:S]),
    }


def reference(x_words, x_scales, w1, w2, w3, wc2, bg2, offs):
    xq = unpack_weight(x_words, x_scales)[:, unstriped(offs)]
    yb = mxq(f64(w1), 0, "e4m3").T @ xq
    yc = mxq(f64(w2), 0, "e4m3").T @ xq
    yg = mxq(f64(w3), 0, "e4m3").T @ xq
    lone = (yb * yc) * sigmoid(yg) + yb
    return lone + (f64(wc2) * (yb * lone)) * (sigmoid(lone + f64(bg2)))

@@ -1,0 +1,144 @@
+from contextlib import ExitStack
+
+import concourse.mybir as mybir
+
+K, T, S, N = 1024, 1024, 512, 128
+FLOPS = 3 * 2 * K * N * S
+
+F32 = mybir.dt.float32
+BF16 = mybir.dt.bfloat16
+I32 = mybir.dt.int32
+U32 = mybir.dt.uint32
+U16 = mybir.dt.uint16
+U8 = mybir.dt.uint8
+FP8X4 = mybir.dt.float8_e4m3fn_x4
+ALU = mybir.AluOpType
+ACT = mybir.ActivationFunctionType
+
+P = 128
+PACK = 4
+PASSES = K // (P * PACK)
+CHUNKS = [(0, 256), (256, 128), (384, 128)]
+CROSS_CHUNKS = [(0, 256), (256, 256)]
+VECTOR_COLS = {("w3", 0): 0, ("w3", 1): 0, ("w2", 0): 128, ("w2", 1): 0, ("w1", 0): 128, ("w1", 1): 80}
+
+
+def tile_picked_ygatcr_two_p_kernel(tc, x_words, x_scales, w1, w2, w3, wc2, bg2, offs, out):
+    nc = tc.nc
+    with ExitStack() as ctx:
+        keep = ctx.enter_context(tc.tile_pool(name="keep", bufs=1))
+        psum = ctx.enter_context(tc.psum_pool(name="psum", bufs=1))
+
+        offsets = keep.tile([P, S // 16], U16, name="offsets")
+        scale_window = keep.tile([P, T], U8, name="scale_window", align_bytes=64)
+        word_window = [keep.tile([P, T], I32, name=f"word_window{g}", align_bytes=64) for g in range(PASSES)]
+        warm = keep.tile([P, 1], F32, name="warm")
+        warm_out = keep.tile([P, 1], F32, name="warm_out")
+
+        nc.vector.memset(scale_window[:].bitcast(I32), 0)
+        nc.vector.memset(warm[:], 0.0)
+        nc.sync.dma_start(offsets[:], offs)
+        scale_queues = [nc.scalar] * 4
+        for q in range(4):
+            scale_queues[q].dma_start(scale_window[32 * q : 32 * q + 8, :].bitcast(I32), x_scales[:, 4 * q : 4 * q + 4, :].bitcast(I32))
+        nc.scalar.activation(warm_out[:], warm[:], ACT.Sigmoid)
+
+        weights = {"w3": w3, "w2": w2, "w1": w1}
+        raw = {}
+        for item in [("x", 0), ("x", 1), ("w3", 0, 1), ("w3", 1, 2), ("w2", 0, 1), ("w2", 1, 2), ("w1", 0, 1), ("w1", 1, 2)]:
+            if item[0] == "x":
+                g = item[1]
+                nc.sync.dma_start(word_window[g][:], x_words[g].rearrange("p n t -> p (n t)").bitcast(I32))
+            else:
+                name, g0, g1 = item
+                tile = keep.tile([P, g1 - g0, PACK, N], F32, name=f"raw_{name}_{g0}")
+                nc.sync.dma_start(tile[:], weights[name].rearrange("(g p j) m -> p g j m", g=PASSES, j=PACK)[:, g0:g1])
+                for g in range(g0, g1):
+                    raw[name, g] = tile[:, g - g0]
+        wc2_col = keep.tile([P, 1], F32, name="wc2_col")
+        bg2_col = keep.tile([P, 1], F32, name="bg2_col")
+        nc.sync.dma_start(bg2_col[:], bg2)
+        nc.sync.dma_start(wc2_col[:], wc2)
+
+        x_codes = [keep.tile([P, S], U32, name=f"x_codes{g}", align_bytes=64) for g in range(PASSES)]
+        x_planes = keep.tile([P, S], U8, name="x_planes", align_bytes=64)
+        nc.vector.tensor_copy(x_planes[:], scale_window[:].indirect(offsets[:]))
+        for g in range(PASSES):
+            nc.vector.tensor_copy(x_codes[g][:], word_window[g][:].bitcast(U32).indirect(offsets[:]))
+
+        grouped, codes, scales = {}, {}, {}
+
+        def cast(name, g):
+            tile = keep.tile([P, N, PACK], BF16, name=f"grouped_{name}_{g}", align_bytes=64)
+            grouped[name, g] = tile
+            split = VECTOR_COLS[name, g]
+            for engine_copy, m0, m1 in ((nc.vector.tensor_copy, 0, split), (nc.scalar.copy, split, N)):
+                if m1 > m0:
+                    engine_copy(
+                        tile[:, m0:m1, :].rearrange("p (c i) j -> p c j i", i=4),
+                        raw[name, g][:, :, m0:m1].rearrange("p j (c i) -> p c j i", i=4),
+                    )
+
+        def quantize(name, g):
+            codes[name, g] = keep.tile([P, N], U32, name=f"codes_{name}_{g}", align_bytes=64)
+            scales[name, g] = keep.tile([P, N], U8, name=f"scales_{name}_{g}", align_bytes=64)
+            nc.vector.quantize_mx(
+                out=codes[name, g][:].bitcast(FP8X4), scales=scales[name, g][:], in_=grouped[name, g][:].rearrange("p m j -> p (m j)")
+            )
+
+        def product(acc, name, g, c0, width):
+            nc.tensor.matmul_mx(
+                out=acc[:],
+                lhsT=codes[name, g][:].bitcast(FP8X4),
+                lhsT_scale=scales[name, g][:],
+                rhs=x_codes[g][:, c0 : c0 + width].bitcast(FP8X4),
+                rhs_scale=x_planes[4 * g : P, c0 : c0 + width],
+                start=(g == 0),
+                stop=(g == PASSES - 1),
+            )
+
+        yg = psum.tile([P, S], F32, name="yg")
+        yc = [psum.tile([P, width], F32, name=f"yc{c}") for c, (c0, width) in enumerate(CROSS_CHUNKS)]
+        yb = [psum.tile([P, width], F32, name=f"yb{c}") for c, (c0, width) in enumerate(CHUNKS)]
+        gate = keep.tile([P, S], F32, name="gate")
+        cross = keep.tile([P, S], F32, name="cross")
+
+        cast("w3", 0)
+        cast("w3", 1)
+        quantize("w3", 0)
+        product(yg, "w3", 0, 0, S)
+        cast("w2", 0)
+        quantize("w3", 1)
+        product(yg, "w3", 1, 0, S)
+        quantize("w2", 0)
+        for c, (c0, width) in enumerate(CROSS_CHUNKS):
+            product(yc[c], "w2", 0, c0, width)
+        cast("w2", 1)
+        nc.scalar.activation(gate[:], yg[:], ACT.Sigmoid)
+        cast("w1", 0)
+        quantize("w2", 1)
+        for c, (c0, width) in enumerate(CROSS_CHUNKS):
+            product(yc[c], "w2", 1, c0, width)
+        quantize("w1", 0)
+        for c, (c0, width) in enumerate(CHUNKS):
+            product(yb[c], "w1", 0, c0, width)
+        cast("w1", 1)
+        quantize("w1", 1)
+        for c, (c0, width) in enumerate(CHUNKS):
+            product(yb[c], "w1", 1, c0, width)
+        for c, (c0, width) in enumerate(CROSS_CHUNKS):
+            nc.vector.tensor_tensor(cross[:, c0 : c0 + width], yc[c][:], gate[:, c0 : c0 + width], ALU.mult)
+
+        lone, gate2, second = [], [], []
+        for c, (c0, width) in enumerate(CHUNKS):
+            lone.append(keep.tile([P, width], F32, name=f"lone{c}"))
+            gate2.append(keep.tile([P, width], F32, name=f"gate2_{c}"))
+            nc.vector.scalar_tensor_tensor(lone[c][:], cross[:, c0 : c0 + width], 1.0, yb[c][:], ALU.add, ALU.mult)
+            nc.scalar.activation(gate2[c][:], lone[c][:], ACT.Sigmoid, bias=bg2_col[:])
+        for c, (c0, width) in enumerate(CHUNKS):
+            second.append(keep.tile([P, width], F32, name=f"second{c}"))
+            nc.vector.scalar_tensor_tensor(second[c][:], yb[c][:], wc2_col[:], gate2[c][:], ALU.mult, ALU.mult)
+        for c, (c0, width) in enumerate(CHUNKS):
+            result = keep.tile([P, width], F32, name=f"result{c}")
+            nc.vector.scalar_tensor_tensor(result[:], second[c][:], 1.0, lone[c][:], ALU.add, ALU.mult)
+            (nc.sync if c % 2 == 0 else nc.scalar).dma_start(out[:, c0 : c0 + width], result[:])

@@ -18,9 +18,8 @@ ACT = mybir.ActivationFunctionType
 P = 128
 PACK = 4
 PASSES = K // (P * PACK)
-CHUNKS = [(0, 256), (256, 128), (384, 128)]
+CHUNKS = [(0, 128), (128, 128), (256, 128), (384, 128)]
 CROSS_CHUNKS = [(0, 256), (256, 256)]
-VECTOR_COLS = {("w3", 0): 0, ("w3", 1): 0, ("w2", 0): 128, ("w2", 1): 0, ("w1", 0): 128, ("w1", 1): 80}
 
 
 def tile_picked_ygatcr_two_p_kernel(tc, x_words, x_scales, w1, w2, w3, wc2, bg2, offs, out):
@@ -34,111 +33,151 @@ def tile_picked_ygatcr_two_p_kernel(tc, x_words, x_scales, w1, w2, w3, wc2, bg2,
         word_window = [keep.tile([P, T], I32, name=f"word_window{g}", align_bytes=64) for g in range(PASSES)]
         warm = keep.tile([P, 1], F32, name="warm")
         warm_out = keep.tile([P, 1], F32, name="warm_out")
+        wc2_col = keep.tile([P, 1], F32, name="wc2_col")
+        bg2_col = keep.tile([P, 1], F32, name="bg2_col")
+        x_codes = [keep.tile([P, S], U32, name=f"x_codes{g}", align_bytes=64) for g in range(PASSES)]
+        x_planes = keep.tile([P, S], U8, name="x_planes", align_bytes=64)
+        weights = {"w3": w3, "w2": w2, "w1": w1}
+        raw, grouped, codes, scales = {}, {}, {}, {}
+
+        def load_scales(queues):
+            for q in range(4):
+                queues[q].dma_start(scale_window[32 * q : 32 * q + 8, :].bitcast(I32), x_scales[:, 4 * q : 4 * q + 4, :].bitcast(I32))
+
+        def load_words(g):
+            nc.sync.dma_start(word_window[g][:], x_words[g].rearrange("p n t -> p (n t)").bitcast(I32))
+
+        def load_weight(name, g0, g1):
+            tile = keep.tile([P, g1 - g0, PACK, N], F32, name=f"raw_{name}_{g0}", tag=f"raw_{name}_{g0}")
+            nc.sync.dma_start(tile[:], weights[name].rearrange("(g p j) m -> p g j m", g=PASSES, j=PACK)[:, g0:g1])
+            for g in range(g0, g1):
+                raw[name, g] = tile[:, g - g0]
+
+        def load_columns(queue):
+            queue.dma_start(bg2_col[:], bg2)
+            queue.dma_start(wc2_col[:], wc2)
+
+        def gather_words(g, c0=0, c1=S):
+            nc.vector.tensor_copy(x_codes[g][:, c0:c1], word_window[g][:].bitcast(U32).indirect(offsets[:, c0 // 16 : c1 // 16]))
+
+        def gather_scales():
+            nc.vector.tensor_copy(x_planes[:], scale_window[:].indirect(offsets[:]))
+
+        def group(*parts):
+            label = "_".join(f"{name}p{g}" for name, g in parts)
+            tile = keep.tile([P, len(parts) * N, PACK], BF16, name=f"grouped_{label}", align_bytes=64)
+            for i, part in enumerate(parts):
+                grouped[part] = tile[:, i * N : (i + 1) * N, :]
+            grouped[parts] = tile
+
+        def cast(name, g, split=0):
+            for engine_copy, m0, m1 in ((nc.vector.tensor_copy, 0, split), (nc.scalar.copy, split, N)):
+                if m1 > m0:
+                    engine_copy(
+                        grouped[name, g][:, m0:m1, :].rearrange("p (c i) j -> p c j i", i=4),
+                        raw[name, g][:, :, m0:m1].rearrange("p j (c i) -> p c j i", i=4),
+                    )
+
+        def quantize(*parts):
+            label = "_".join(f"{name}p{g}" for name, g in parts)
+            words = keep.tile([P, len(parts) * N], U32, name=f"codes_{label}", align_bytes=64)
+            plane = keep.tile([P, len(parts) * N], U8, name=f"scales_{label}", align_bytes=64)
+            nc.vector.quantize_mx(out=words[:].bitcast(FP8X4), scales=plane[:], in_=grouped[parts][:].rearrange("p m j -> p (m j)"))
+            for i, part in enumerate(parts):
+                codes[part] = words[:, i * N : (i + 1) * N]
+                scales[part] = plane[:, i * N : (i + 1) * N]
+
+        yg = [psum.tile([P, width], F32, name=f"yg{c}") for c, (c0, width) in enumerate(CROSS_CHUNKS)]
+        yc = [psum.tile([P, width], F32, name=f"yc{c}") for c, (c0, width) in enumerate(CROSS_CHUNKS)]
+        yb = [psum.tile([P, width], F32, name=f"yb{c}") for c, (c0, width) in enumerate(CHUNKS)]
+        banks = {"w3": (yg, CROSS_CHUNKS), "w2": (yc, CROSS_CHUNKS), "w1": (yb, CHUNKS)}
+        cross = keep.tile([P, S], F32, name="cross")
+
+        def products(name, g):
+            for acc, (c0, width) in zip(*banks[name]):
+                nc.tensor.matmul_mx(
+                    out=acc[:],
+                    lhsT=codes[name, g].bitcast(FP8X4),
+                    lhsT_scale=scales[name, g],
+                    rhs=x_codes[g][:, c0 : c0 + width].bitcast(FP8X4),
+                    rhs_scale=x_planes[4 * g : P, c0 : c0 + width],
+                    start=(g == 0),
+                    stop=(g == PASSES - 1),
+                )
+
+        def first_gate(c):
+            c0, width = CROSS_CHUNKS[c]
+            nc.scalar.activation(gate[:, c0 : c0 + width], yg[c][:], ACT.Sigmoid)
+
+        def first_cross(c):
+            c0, width = CROSS_CHUNKS[c]
+            nc.vector.tensor_tensor(cross[:, c0 : c0 + width], yc[c][:], gate[:, c0 : c0 + width], ALU.mult)
+
+        lone, gate2, second = {}, {}, {}
+
+        def step_lone(c):
+            c0, width = CHUNKS[c]
+            lone[c] = keep.tile([P, width], F32, name=f"lone{c}")
+            gate2[c] = keep.tile([P, width], F32, name=f"gate2_{c}")
+            nc.vector.scalar_tensor_tensor(lone[c][:], cross[:, c0 : c0 + width], 1.0, yb[c][:], ALU.add, ALU.mult)
+            nc.scalar.activation(gate2[c][:], lone[c][:], ACT.Sigmoid, bias=bg2_col[:])
+
+        def step_second(c):
+            c0, width = CHUNKS[c]
+            second[c] = keep.tile([P, width], F32, name=f"second{c}")
+            nc.vector.scalar_tensor_tensor(second[c][:], yb[c][:], wc2_col[:], gate2[c][:], ALU.mult, ALU.mult)
+
+        def step_out(c, queue):
+            c0, width = CHUNKS[c]
+            result = keep.tile([P, width], F32, name=f"result{c}")
+            nc.vector.scalar_tensor_tensor(result[:], second[c][:], 1.0, lone[c][:], ALU.add, ALU.mult)
+            queue.dma_start(out[:, c0 : c0 + width], result[:])
 
         nc.vector.memset(scale_window[:].bitcast(I32), 0)
         nc.vector.memset(warm[:], 0.0)
         nc.sync.dma_start(offsets[:], offs)
-        scale_queues = [nc.scalar] * 4
-        for q in range(4):
-            scale_queues[q].dma_start(scale_window[32 * q : 32 * q + 8, :].bitcast(I32), x_scales[:, 4 * q : 4 * q + 4, :].bitcast(I32))
+        load_words(0)
+        load_scales([nc.sync] * 4)
         nc.scalar.activation(warm_out[:], warm[:], ACT.Sigmoid)
-
-        weights = {"w3": w3, "w2": w2, "w1": w1}
-        raw = {}
-        for item in [("x", 0), ("x", 1), ("w3", 0, 1), ("w3", 1, 2), ("w2", 0, 1), ("w2", 1, 2), ("w1", 0, 1), ("w1", 1, 2)]:
-            if item[0] == "x":
-                g = item[1]
-                nc.sync.dma_start(word_window[g][:], x_words[g].rearrange("p n t -> p (n t)").bitcast(I32))
-            else:
-                name, g0, g1 = item
-                tile = keep.tile([P, g1 - g0, PACK, N], F32, name=f"raw_{name}_{g0}")
-                nc.sync.dma_start(tile[:], weights[name].rearrange("(g p j) m -> p g j m", g=PASSES, j=PACK)[:, g0:g1])
-                for g in range(g0, g1):
-                    raw[name, g] = tile[:, g - g0]
-        wc2_col = keep.tile([P, 1], F32, name="wc2_col")
-        bg2_col = keep.tile([P, 1], F32, name="bg2_col")
-        nc.sync.dma_start(bg2_col[:], bg2)
-        nc.sync.dma_start(wc2_col[:], wc2)
-
-        x_codes = [keep.tile([P, S], U32, name=f"x_codes{g}", align_bytes=64) for g in range(PASSES)]
-        x_planes = keep.tile([P, S], U8, name="x_planes", align_bytes=64)
-        nc.vector.tensor_copy(x_planes[:], scale_window[:].indirect(offsets[:]))
-        for g in range(PASSES):
-            nc.vector.tensor_copy(x_codes[g][:], word_window[g][:].bitcast(U32).indirect(offsets[:]))
-
-        grouped, codes, scales = {}, {}, {}
-
-        def cast(name, g):
-            tile = keep.tile([P, N, PACK], BF16, name=f"grouped_{name}_{g}", align_bytes=64)
-            grouped[name, g] = tile
-            split = VECTOR_COLS[name, g]
-            for engine_copy, m0, m1 in ((nc.vector.tensor_copy, 0, split), (nc.scalar.copy, split, N)):
-                if m1 > m0:
-                    engine_copy(
-                        tile[:, m0:m1, :].rearrange("p (c i) j -> p c j i", i=4),
-                        raw[name, g][:, :, m0:m1].rearrange("p j (c i) -> p c j i", i=4),
-                    )
-
-        def quantize(name, g):
-            codes[name, g] = keep.tile([P, N], U32, name=f"codes_{name}_{g}", align_bytes=64)
-            scales[name, g] = keep.tile([P, N], U8, name=f"scales_{name}_{g}", align_bytes=64)
-            nc.vector.quantize_mx(
-                out=codes[name, g][:].bitcast(FP8X4), scales=scales[name, g][:], in_=grouped[name, g][:].rearrange("p m j -> p (m j)")
-            )
-
-        def product(acc, name, g, c0, width):
-            nc.tensor.matmul_mx(
-                out=acc[:],
-                lhsT=codes[name, g][:].bitcast(FP8X4),
-                lhsT_scale=scales[name, g][:],
-                rhs=x_codes[g][:, c0 : c0 + width].bitcast(FP8X4),
-                rhs_scale=x_planes[4 * g : P, c0 : c0 + width],
-                start=(g == 0),
-                stop=(g == PASSES - 1),
-            )
-
-        yg = psum.tile([P, S], F32, name="yg")
-        yc = [psum.tile([P, width], F32, name=f"yc{c}") for c, (c0, width) in enumerate(CROSS_CHUNKS)]
-        yb = [psum.tile([P, width], F32, name=f"yb{c}") for c, (c0, width) in enumerate(CHUNKS)]
-        gate = keep.tile([P, S], F32, name="gate")
-        cross = keep.tile([P, S], F32, name="cross")
-
+        load_weight("w3", 0, 1)
+        load_weight("w2", 0, 1)
+        load_words(1)
+        load_weight("w3", 1, 2)
+        load_weight("w2", 1, 2)
+        load_weight("w1", 0, 1)
+        load_weight("w1", 1, 2)
+        load_columns(nc.sync)
+        group(("w3", 0), ("w2", 0))
+        for part in (("w3", 1), ("w2", 1), ("w1", 0), ("w1", 1)):
+            group(part)
+        gather_words(0)
+        gather_scales()
         cast("w3", 0)
-        cast("w3", 1)
-        quantize("w3", 0)
-        product(yg, "w3", 0, 0, S)
         cast("w2", 0)
-        quantize("w3", 1)
-        product(yg, "w3", 1, 0, S)
-        quantize("w2", 0)
-        for c, (c0, width) in enumerate(CROSS_CHUNKS):
-            product(yc[c], "w2", 0, c0, width)
+        quantize(("w3", 0), ("w2", 0))
+        products("w3", 0)
+        products("w2", 0)
+        gather_words(1)
+        cast("w3", 1)
         cast("w2", 1)
-        nc.scalar.activation(gate[:], yg[:], ACT.Sigmoid)
         cast("w1", 0)
-        quantize("w2", 1)
-        for c, (c0, width) in enumerate(CROSS_CHUNKS):
-            product(yc[c], "w2", 1, c0, width)
-        quantize("w1", 0)
-        for c, (c0, width) in enumerate(CHUNKS):
-            product(yb[c], "w1", 0, c0, width)
-        cast("w1", 1)
-        quantize("w1", 1)
-        for c, (c0, width) in enumerate(CHUNKS):
-            product(yb[c], "w1", 1, c0, width)
-        for c, (c0, width) in enumerate(CROSS_CHUNKS):
-            nc.vector.tensor_tensor(cross[:, c0 : c0 + width], yc[c][:], gate[:, c0 : c0 + width], ALU.mult)
-
-        lone, gate2, second = [], [], []
-        for c, (c0, width) in enumerate(CHUNKS):
-            lone.append(keep.tile([P, width], F32, name=f"lone{c}"))
-            gate2.append(keep.tile([P, width], F32, name=f"gate2_{c}"))
-            nc.vector.scalar_tensor_tensor(lone[c][:], cross[:, c0 : c0 + width], 1.0, yb[c][:], ALU.add, ALU.mult)
-            nc.scalar.activation(gate2[c][:], lone[c][:], ACT.Sigmoid, bias=bg2_col[:])
-        for c, (c0, width) in enumerate(CHUNKS):
-            second.append(keep.tile([P, width], F32, name=f"second{c}"))
-            nc.vector.scalar_tensor_tensor(second[c][:], yb[c][:], wc2_col[:], gate2[c][:], ALU.mult, ALU.mult)
-        for c, (c0, width) in enumerate(CHUNKS):
-            result = keep.tile([P, width], F32, name=f"result{c}")
-            nc.vector.scalar_tensor_tensor(result[:], second[c][:], 1.0, lone[c][:], ALU.add, ALU.mult)
-            (nc.sync if c % 2 == 0 else nc.scalar).dma_start(out[:, c0 : c0 + width], result[:])
+        quantize(("w3", 1))
+        products("w3", 1)
+        quantize(("w2", 1))
+        products("w2", 1)
+        cast("w1", 1, 128)
+        quantize(("w1", 0))
+        products("w1", 0)
+        gate = keep.tile([P, S], F32, name="gate", tag="raw_w1_0")
+        first_gate(0)
+        first_gate(1)
+        quantize(("w1", 1))
+        products("w1", 1)
+        first_cross(0)
+        first_cross(1)
+        for c in range(4):
+            step_lone(c)
+        for c in range(4):
+            step_second(c)
+        for c in range(4):
+            step_out(c, nc.scalar if c == 3 else nc.sync)

from contextlib import ExitStack

import concourse.mybir as mybir

K, T, S, N = 1024, 1024, 512, 128
FLOPS = 3 * 2 * K * N * S

F32 = mybir.dt.float32
BF16 = mybir.dt.bfloat16
I32 = mybir.dt.int32
U32 = mybir.dt.uint32
U16 = mybir.dt.uint16
U8 = mybir.dt.uint8
FP8X4 = mybir.dt.float8_e4m3fn_x4
ALU = mybir.AluOpType
ACT = mybir.ActivationFunctionType

P = 128
PACK = 4
PASSES = K // (P * PACK)
CHUNKS = [(0, 128), (128, 128), (256, 128), (384, 128)]
CROSS_CHUNKS = [(0, 256), (256, 256)]


def tile_picked_ygatcr_two_p_kernel(tc, x_words, x_scales, w1, w2, w3, wc2, bg2, offs, out):
    nc = tc.nc
    with ExitStack() as ctx:
        keep = ctx.enter_context(tc.tile_pool(name="keep", bufs=1))
        psum = ctx.enter_context(tc.psum_pool(name="psum", bufs=1))

        offsets = keep.tile([P, S // 16], U16, name="offsets")
        scale_window = keep.tile([P, T], U8, name="scale_window", align_bytes=64)
        word_window = [keep.tile([P, T], I32, name=f"word_window{g}", align_bytes=64) for g in range(PASSES)]
        warm = keep.tile([P, 1], F32, name="warm")
        warm_out = keep.tile([P, 1], F32, name="warm_out")
        wc2_col = keep.tile([P, 1], F32, name="wc2_col")
        bg2_col = keep.tile([P, 1], F32, name="bg2_col")
        x_codes = [keep.tile([P, S], U32, name=f"x_codes{g}", align_bytes=64) for g in range(PASSES)]
        x_planes = keep.tile([P, S], U8, name="x_planes", align_bytes=64)
        weights = {"w3": w3, "w2": w2, "w1": w1}
        raw, grouped, codes, scales = {}, {}, {}, {}

        def load_scales(queues):
            for q in range(4):
                queues[q].dma_start(scale_window[32 * q : 32 * q + 8, :].bitcast(I32), x_scales[:, 4 * q : 4 * q + 4, :].bitcast(I32))

        def load_words(g):
            nc.sync.dma_start(word_window[g][:], x_words[g].rearrange("p n t -> p (n t)").bitcast(I32))

        def load_weight(name, g0, g1):
            tile = keep.tile([P, g1 - g0, PACK, N], F32, name=f"raw_{name}_{g0}", tag=f"raw_{name}_{g0}")
            nc.sync.dma_start(tile[:], weights[name].rearrange("(g p j) m -> p g j m", g=PASSES, j=PACK)[:, g0:g1])
            for g in range(g0, g1):
                raw[name, g] = tile[:, g - g0]

        def load_columns(queue):
            queue.dma_start(bg2_col[:], bg2)
            queue.dma_start(wc2_col[:], wc2)

        def gather_words(g, c0=0, c1=S):
            nc.vector.tensor_copy(x_codes[g][:, c0:c1], word_window[g][:].bitcast(U32).indirect(offsets[:, c0 // 16 : c1 // 16]))

        def gather_scales():
            nc.vector.tensor_copy(x_planes[:], scale_window[:].indirect(offsets[:]))

        def group(*parts):
            label = "_".join(f"{name}p{g}" for name, g in parts)
            tile = keep.tile([P, len(parts) * N, PACK], BF16, name=f"grouped_{label}", align_bytes=64)
            for i, part in enumerate(parts):
                grouped[part] = tile[:, i * N : (i + 1) * N, :]
            grouped[parts] = tile

        def cast(name, g, split=0):
            for engine_copy, m0, m1 in ((nc.vector.tensor_copy, 0, split), (nc.scalar.copy, split, N)):
                if m1 > m0:
                    engine_copy(
                        grouped[name, g][:, m0:m1, :].rearrange("p (c i) j -> p c j i", i=4),
                        raw[name, g][:, :, m0:m1].rearrange("p j (c i) -> p c j i", i=4),
                    )

        def quantize(*parts):
            label = "_".join(f"{name}p{g}" for name, g in parts)
            words = keep.tile([P, len(parts) * N], U32, name=f"codes_{label}", align_bytes=64)
            plane = keep.tile([P, len(parts) * N], U8, name=f"scales_{label}", align_bytes=64)
            nc.vector.quantize_mx(out=words[:].bitcast(FP8X4), scales=plane[:], in_=grouped[parts][:].rearrange("p m j -> p (m j)"))
            for i, part in enumerate(parts):
                codes[part] = words[:, i * N : (i + 1) * N]
                scales[part] = plane[:, i * N : (i + 1) * N]

        yg = [psum.tile([P, width], F32, name=f"yg{c}") for c, (c0, width) in enumerate(CROSS_CHUNKS)]
        yc = [psum.tile([P, width], F32, name=f"yc{c}") for c, (c0, width) in enumerate(CROSS_CHUNKS)]
        yb = [psum.tile([P, width], F32, name=f"yb{c}") for c, (c0, width) in enumerate(CHUNKS)]
        banks = {"w3": (yg, CROSS_CHUNKS), "w2": (yc, CROSS_CHUNKS), "w1": (yb, CHUNKS)}
        cross = keep.tile([P, S], F32, name="cross")

        def products(name, g):
            for acc, (c0, width) in zip(*banks[name]):
                nc.tensor.matmul_mx(
                    out=acc[:],
                    lhsT=codes[name, g].bitcast(FP8X4),
                    lhsT_scale=scales[name, g],
                    rhs=x_codes[g][:, c0 : c0 + width].bitcast(FP8X4),
                    rhs_scale=x_planes[4 * g : P, c0 : c0 + width],
                    start=(g == 0),
                    stop=(g == PASSES - 1),
                )

        def first_gate(c):
            c0, width = CROSS_CHUNKS[c]
            nc.scalar.activation(gate[:, c0 : c0 + width], yg[c][:], ACT.Sigmoid)

        def first_cross(c):
            c0, width = CROSS_CHUNKS[c]
            nc.vector.tensor_tensor(cross[:, c0 : c0 + width], yc[c][:], gate[:, c0 : c0 + width], ALU.mult)

        lone, gate2, second = {}, {}, {}

        def step_lone(c):
            c0, width = CHUNKS[c]
            lone[c] = keep.tile([P, width], F32, name=f"lone{c}")
            gate2[c] = keep.tile([P, width], F32, name=f"gate2_{c}")
            nc.vector.scalar_tensor_tensor(lone[c][:], cross[:, c0 : c0 + width], 1.0, yb[c][:], ALU.add, ALU.mult)
            nc.scalar.activation(gate2[c][:], lone[c][:], ACT.Sigmoid, bias=bg2_col[:])

        def step_second(c):
            c0, width = CHUNKS[c]
            second[c] = keep.tile([P, width], F32, name=f"second{c}")
            nc.vector.scalar_tensor_tensor(second[c][:], yb[c][:], wc2_col[:], gate2[c][:], ALU.mult, ALU.mult)

        def step_out(c, queue):
            c0, width = CHUNKS[c]
            result = keep.tile([P, width], F32, name=f"result{c}")
            nc.vector.scalar_tensor_tensor(result[:], second[c][:], 1.0, lone[c][:], ALU.add, ALU.mult)
            queue.dma_start(out[:, c0 : c0 + width], result[:])

        nc.vector.memset(scale_window[:].bitcast(I32), 0)
        nc.vector.memset(warm[:], 0.0)
        nc.sync.dma_start(offsets[:], offs)
        load_words(0)
        load_scales([nc.sync] * 4)
        nc.scalar.activation(warm_out[:], warm[:], ACT.Sigmoid)
        load_weight("w3", 0, 1)
        load_weight("w2", 0, 1)
        load_words(1)
        load_weight("w3", 1, 2)
        load_weight("w2", 1, 2)
        load_weight("w1", 0, 1)
        load_weight("w1", 1, 2)
        load_columns(nc.sync)
        group(("w3", 0), ("w2", 0))
        for part in (("w3", 1), ("w2", 1), ("w1", 0), ("w1", 1)):
            group(part)
        gather_words(0)
        gather_scales()
        cast("w3", 0)
        cast("w2", 0)
        quantize(("w3", 0), ("w2", 0))
        products("w3", 0)
        products("w2", 0)
        gather_words(1)
        cast("w3", 1)
        cast("w2", 1)
        cast("w1", 0)
        quantize(("w3", 1))
        products("w3", 1)
        quantize(("w2", 1))
        products("w2", 1)
        cast("w1", 1, 128)
        quantize(("w1", 0))
        products("w1", 0)
        gate = keep.tile([P, S], F32, name="gate", tag="raw_w1_0")
        first_gate(0)
        first_gate(1)
        quantize(("w1", 1))
        products("w1", 1)
        first_cross(0)
        first_cross(1)
        for c in range(4):
            step_lone(c)
        for c in range(4):
            step_second(c)
        for c in range(4):
            step_out(c, nc.scalar if c == 3 else nc.sync)
